import numpy as np, ml_dtypes
CORES = [24,32,56,88,96,104,30,38,62,94,102,110]
N = 12
QP = 64
def setup_inputs(rng):
    m = 150 * rng.standard_normal((1, QP, 1), dtype=np.float32) + 3 * rng.standard_normal((N, QP, 1), dtype=np.float32)
    m = (m + rng.uniform(100, 300, (1, QP, 1)) * (rng.random((1, QP, 1)) < 0.7) * (rng.random((N, QP, 1)) < 0.5)).astype(np.float32)
    l = 20 * (1 + np.abs(rng.standard_normal((N, QP, 1), dtype=np.float32)))
    return {"o": (l * rng.standard_normal((N, QP, 128), dtype=np.float32) / 4).astype(ml_dtypes.bfloat16), "ml": np.concatenate([m, l], axis=2)}
def setup_inputs_big(rng):
    d = setup_inputs(rng)
    for k in ("o",): d[k] = (d[k].astype(np.float32) * 1048576.0).astype(d[k].dtype)
    return d
def setup_inputs_small(rng):
    d = setup_inputs(rng)
    for k in ("o",): d[k] = (d[k].astype(np.float32) * (1 / 1048576.0)).astype(d[k].dtype)
    return d
def reference(o, ml):
    O, ML = o.astype(np.float64), ml.astype(np.float64)
    m, l = ML[:, :, 0:1], ML[:, :, 1:2]
    f = np.exp(m - m.max(axis=0))
    y = ((f * O).sum(axis=0) / (f * l).sum(axis=0)).astype(ml_dtypes.bfloat16)
    return {"y": np.broadcast_to(y, (N,) + y.shape)}

@@ -1,0 +1,173 @@
+from concourse.bass import DstId, RemoteDMATransfer
+from concourse.mybir import AluOpType, AxisListType, ActivationFunctionType
+
+N = 12
+Q = 64
+NCH = N // 2
+W = 136
+
+SCRATCH = {
+    "land_o": ("dram", [N, 128, 64], "bfloat16"),
+    "land_ml": ("dram", [N, 128, 2], "float32"),
+    "mlb": ("sbuf", [128, 256], "float32"),
+    "o_all": ("sbuf", [128, NCH * W], "bfloat16"),
+    "ones": ("sbuf", [128, 128], "float32"),
+    "ident": ("sbuf", [128, 128], "float32"),
+    "istack": ("sbuf", [128, 64], "bfloat16"),
+    "amat": ("sbuf", [128, NCH * 64], "bfloat16"),
+    "negm": ("sbuf", [128, 1], "float32"),
+    "fsel": ("sbuf", [128, 8], "float32"),
+    "rden": ("sbuf", [128, 1], "float32"),
+    "y_sb": ("sbuf", [128, 128], "bfloat16"),
+    "ps_m": ("psum", [128, 512], "float32"),
+    "ps_l": ("psum", [128, 512], "float32"),
+    "ps_y": ("psum", [128, 512], "float32"),
+}
+SEMAPHORES = (["ld_ml", "ld_o", "ml_sib", "ml_arr", "o_sib", "sent", "k_ones", "k_id", "k_is", "ml_in", "pm", "pl",
+               "vm", "vl", "sf", "py", "vr", "vy", "st"]
+              + ["o_c%d" % k for k in range(NCH)] + ["c%d" % k for k in range(NCH)] + ["a%d" % k for k in range(NCH)])
+
+NE_O, NE_RO, NE_SO = 4, 4, 2
+
+
+def _bits(mask):
+    return [e for e in range(mask.bit_length()) if (mask >> e) & 1]
+
+
+def _mk(engs):
+    return sum(1 << e for e in engs)
+
+
+def rank_program(g, core, T, topo):
+    if T.rank_of(core) is None:
+        return
+    cores = list(T.cores)
+    sem = T.sem
+
+    def reach(s):
+        return tuple(bool(s == d or topo.may_write(s, d)) for d in cores)
+
+    order = sorted(cores, key=lambda s: (reach(s), cores.index(s)))
+    slot = {s: i for i, s in enumerate(order)}
+
+    def sib_of(c):
+        return [x for x in cores if x != c and topo.chip(x) == topo.chip(c)][0]
+
+    sib = sib_of(core)
+    others = [d for d in cores if d != core and d != sib]
+    direct = [d for d in others if topo.may_write(core, d)]
+    passed = [d for d in others if not topo.may_write(sib, d)]
+    off = _bits(topo.mask(core, others[0]))
+    on_only = [e for e in _bits(topo.mask(core, sib)) if e not in off]
+    e_o, e_ro = off[0:NE_O], off[4:4 + NE_RO]
+    e_m = [off[4], off[6]]
+    e_sm, e_so = [on_only[0]], [on_only[0], on_only[2]]
+    me = slot[core]
+    sent = [0]
+
+    def xfer(buf, s, dests, engs, rsem):
+        ids = []
+        for d in dests:
+            rid, pid, _ = topo.addr(d)
+            ids.append(DstId(rid=rid, pnc=pid))
+        sent[0] += len(engs)
+        return RemoteDMATransfer(dst_ids=ids, dma_engine_mask=_mk(engs), remote_sem=rsem, srcs=[buf[s]],
+                                 dsts=[buf[s]] * len(dests), alu_op=0)
+
+    def ml_xfers(s, dests):
+        return [xfer(T.land_ml, s, part, [e], sem.ml_arr)
+                for part, e in ((dests[0::2], e_m[0]), (dests[1::2], e_m[1])) if part]
+
+    g.sync.dma_start(T.land_ml[me, 0:64, :], T.ml[:]).then_inc(sem.ld_ml, 16)
+    g.scalar.dma_start(T.land_ml[me, 64:128, :], T.ml[:]).then_inc(sem.ld_ml, 16)
+    g.sync.dma_start(T.land_o[me], T.o[:]).then_inc(sem.ld_o, 16)
+
+    g.vector.memset(T.ones[:], 1.0).then_inc(sem.k_ones, 1)
+    g.wait_ge(sem.k_ones, 1)
+    g.affine_select(T.ident[:], T.ones[:], [[-1, 128]], AluOpType.is_equal, 0.0, 0, 1).then_inc(sem.k_id, 1)
+    g.vector.wait_ge(sem.k_id, 1)
+    g.vector.tensor_tensor(T.istack[:], T.ident[:, 0:64], T.ident[:, 64:128], AluOpType.add).then_inc(sem.k_is, 1)
+
+    g.wait_ge(sem.ld_ml, 32)
+    g.remote_dma_fused([xfer(T.land_ml, me, [sib], e_sm, sem.ml_sib)] + ml_xfers(me, direct), local_sem=sem.sent)
+    g.wait_ge(sem.ld_o, 16)
+    g.remote_dma_fused([xfer(T.land_o, me, [sib], e_so, sem.o_sib),
+                        xfer(T.land_o, me, direct, e_o, sem["o_c%d" % (me // 2)])], local_sem=sem.sent)
+    if passed:
+        ss = slot[sib]
+        g.wait_ge(sem.ml_sib, 1)
+        g.remote_dma_fused(ml_xfers(ss, passed), local_sem=sem.sent)
+        g.wait_ge(sem.o_sib, NE_SO)
+        g.remote_dma_fused([xfer(T.land_o, ss, passed, e_ro, sem["o_c%d" % (ss // 2)])], local_sem=sem.sent)
+    g.wait_ge(sem.sent, sent[0])
+
+    g.scalar.wait_ge(sem.ld_ml, 32)
+    g.scalar.wait_ge(sem.ml_sib, 1)
+    g.scalar.wait_ge(sem.ml_arr, len(others))
+    g.scalar.dma_start(T.mlb[0:N, :], T.land_ml[:]).then_inc(sem.ml_in, 16)
+
+    def late(k):
+        return any(not (s == core or topo.may_write(s, core)) for s in order[2 * k:2 * k + 2])
+
+    korder = sorted(range(NCH), key=lambda k: (late(k), k))
+    for k in korder:
+        cnt = 0
+        for s in order[2 * k:2 * k + 2]:
+            if s == core:
+                g.sync.wait_ge(sem.ld_o, 16)
+            elif s == sib:
+                g.sync.wait_ge(sem.o_sib, NE_SO)
+            else:
+                cnt += NE_O if topo.may_write(s, core) else NE_RO
+        if cnt:
+            g.sync.wait_ge(sem["o_c%d" % k], cnt)
+        g.sync.dma_start(T.o_all[:, k * W:k * W + 128], T.land_o[2 * k:2 * k + 2]).then_inc(sem["c%d" % k], 16)
+
+    g.tensor.wait_ge(sem.k_id, 1)
+    g.tensor.wait_ge(sem.ml_in, 16)
+    g.tensor.matmul(T.ps_m[:, 0:N], T.mlb[0:N, 0:256:2], T.ident[0:N, 0:N], True, True).then_inc(sem.pm, 1)
+    g.tensor.matmul(T.ps_l[:, 0:N], T.mlb[0:N, 1:256:2], T.ident[0:N, 0:N], True, True).then_inc(sem.pl, 1)
+
+    g.vector.wait_ge(sem.pm, 1)
+    g.vector.tensor_reduce(T.negm[:, 0:1], T.ps_m[:, 0:N], AxisListType.X, AluOpType.max,
+                           negate=True).then_inc(sem.vm, 1)
+    g.vector.wait_ge(sem.pl, 1)
+    for h in (0, 1):
+        g.vector.tensor_copy(T.o_all[64 * h:64 * h + 64, 128:NCH * W:W],
+                             T.ps_l[64 * h:64 * h + 64, h:N:2]).then_inc(sem.vl, 1)
+
+    g.scalar.wait_ge(sem.vm, 1)
+    for h in (0, 1):
+        g.scalar.activation(T.fsel[64 * h:64 * h + 64, 0:NCH], T.ps_m[64 * h:64 * h + 64, h:N:2],
+                            ActivationFunctionType.Exp, bias=T.negm[64 * h:64 * h + 64, 0:1],
+                            scale=1.0).then_inc(sem.sf, 1)
+
+    g.vector.wait_ge(sem.sf, 2)
+    g.vector.wait_ge(sem.k_is, 1)
+    g.scalar.wait_ge(sem.sf, 2)
+    g.scalar.wait_ge(sem.k_is, 1)
+    for i, k in enumerate(korder):
+        a_k = T.amat[:, 64 * k:64 * k + 64]
+        if i % 2 == 0:
+            g.vector.tensor_scalar(a_k, T.istack[:], T.fsel[:, k:k + 1], None,
+                                   AluOpType.mult).then_inc(sem["a%d" % k], 1)
+        else:
+            g.scalar.activation(a_k, T.istack[:], ActivationFunctionType.Copy,
+                                scale=T.fsel[:, k:k + 1]).then_inc(sem["a%d" % k], 1)
+
+    g.tensor.wait_ge(sem.vl, 2)
+    for i, k in enumerate(korder):
+        g.tensor.wait_ge(sem["a%d" % k], 1)
+        g.tensor.wait_ge(sem["c%d" % k], 16)
+        mm = g.tensor.matmul(T.ps_y[0:Q, 0:129], T.amat[:, 64 * k:64 * k + 64], T.o_all[:, k * W:k * W + 129],
+                             i == 0, i == NCH - 1)
+    mm.then_inc(sem.py, 1)
+
+    g.vector.wait_ge(sem.py, 1)
+    g.vector.reciprocal(T.rden[0:Q, 0:1], T.ps_y[0:Q, 128:129]).then_inc(sem.vr, 1)
+    g.vector.wait_ge(sem.vr, 1)
+    g.vector.tensor_scalar(T.y_sb[0:Q, :], T.ps_y[0:Q, 0:128], T.rden[0:Q, 0:1], None,
+                           AluOpType.mult).then_inc(sem.vy, 1)
+    g.sync.wait_ge(sem.vy, 1)
+    g.sync.dma_start(T.y[:], T.y_sb[0:Q, :]).then_inc(sem.st, 16)
+    g.sync.wait_ge(sem.st, 16)

@@ -9,25 +9,32 @@ W = 136
 SCRATCH = {
     "land_o": ("dram", [N, 128, 64], "bfloat16"),
     "land_ml": ("dram", [N, 128, 2], "float32"),
-    "mlb": ("sbuf", [128, 256], "float32"),
+    "mlb_e": ("sbuf", [128, 256], "float32"),
+    "mlb_t": ("sbuf", [128, 256], "float32"),
     "o_all": ("sbuf", [128, NCH * W], "bfloat16"),
     "ones": ("sbuf", [128, 128], "float32"),
     "ident": ("sbuf", [128, 128], "float32"),
     "istack": ("sbuf", [128, 64], "bfloat16"),
     "amat": ("sbuf", [128, NCH * 64], "bfloat16"),
+    "negm_e": ("sbuf", [128, 1], "float32"),
     "negm": ("sbuf", [128, 1], "float32"),
-    "fsel": ("sbuf", [128, 8], "float32"),
+    "f_e": ("sbuf", [128, 8], "float32"),
+    "f_t": ("sbuf", [128, 8], "float32"),
     "rden": ("sbuf", [128, 1], "float32"),
     "y_sb": ("sbuf", [128, 128], "bfloat16"),
-    "ps_m": ("psum", [128, 512], "float32"),
-    "ps_l": ("psum", [128, 512], "float32"),
+    "ps_me": ("psum", [128, 512], "float32"),
+    "ps_le": ("psum", [128, 512], "float32"),
+    "ps_mt": ("psum", [128, 512], "float32"),
+    "ps_lt": ("psum", [128, 512], "float32"),
     "ps_y": ("psum", [128, 512], "float32"),
 }
-SEMAPHORES = (["ld_ml", "ld_o", "ml_sib", "ml_arr", "o_sib", "sent", "k_ones", "k_id", "k_is", "ml_in", "pm", "pl",
-               "vm", "vl", "sf", "py", "vr", "vy", "st"]
+SEMAPHORES = (["ld_ml", "ld_o", "ml_sib", "ml_arr", "ml_late", "o_sib", "sent", "k_ones", "k_id", "k_is",
+               "mle_in", "mlt_in", "pme", "ple", "pmt", "plt", "vme", "vme2", "vle", "vmt", "vlt", "sfe",
+               "sft", "py", "vr", "vy", "st"]
               + ["o_c%d" % k for k in range(NCH)] + ["c%d" % k for k in range(NCH)] + ["a%d" % k for k in range(NCH)])
 
-NE_O, NE_RO, NE_SO = 4, 4, 2
+NE_O, NE_RO, NE_SO = 4, 4, 4
+NHELP = 2
 
 
 def _bits(mask):
@@ -39,48 +46,92 @@ def _mk(engs):
 
 
 def rank_program(g, core, T, topo):
-    if T.rank_of(core) is None:
-        return
     cores = list(T.cores)
     sem = T.sem
+    Exp, Copy = ActivationFunctionType.Exp, ActivationFunctionType.Copy
+    mult = AluOpType.mult
 
-    def reach(s):
-        return tuple(bool(s == d or topo.may_write(s, d)) for d in cores)
+    def hop1(s, d):
+        return bool(s == d or topo.may_write(s, d))
 
-    order = sorted(cores, key=lambda s: (reach(s), cores.index(s)))
-    slot = {s: i for i, s in enumerate(order)}
+    gorder = sorted(cores, key=lambda s: (tuple(hop1(s, d) for d in cores), cores.index(s)))
+    gidx = {s: i for i, s in enumerate(gorder)}
 
-    def sib_of(c):
-        return [x for x in cores if x != c and topo.chip(x) == topo.chip(c)][0]
+    def order_of(d):
+        return sorted(cores, key=lambda s: (not hop1(s, d), gidx[s]))
 
-    sib = sib_of(core)
-    others = [d for d in cores if d != core and d != sib]
-    direct = [d for d in others if topo.may_write(core, d)]
-    passed = [d for d in others if not topo.may_write(sib, d)]
-    off = _bits(topo.mask(core, others[0]))
-    on_only = [e for e in _bits(topo.mask(core, sib)) if e not in off]
-    e_o, e_ro = off[0:NE_O], off[4:4 + NE_RO]
-    e_m = [off[4], off[6]]
-    e_sm, e_so = [on_only[0]], [on_only[0], on_only[2]]
-    me = slot[core]
+    def n_early(d):
+        return sum(1 for s in cores if hop1(s, d))
+
+    def oslot(d, s):
+        return order_of(d).index(s) if d in cores else 0
+
+    def mslot(d, s):
+        j, ne = oslot(d, s), n_early(d)
+        if j < ne:
+            return (j % 2) * (ne // 2) + j // 2
+        j -= ne
+        return ne + (j % 2) * ((N - ne) // 2) + j // 2
+
+    def unreached(s):
+        return [d for d in cores if not hop1(s, d)]
+
+    def helpers(s):
+        far = unreached(s)
+        if not far:
+            return []
+        return [c for c in range(topo.CORES_PER_CHIP * topo.CHIPS)
+                if c not in cores and topo.chip(c) == topo.chip(s) and topo.die(c) == topo.die(s)
+                and all(topo.may_write(c, d) for d in far)][:NHELP]
+
     sent = [0]
 
-    def xfer(buf, s, dests, engs, rsem):
+    def xfer(buf, slot_fn, s, dests, engs, rsem):
         ids = []
         for d in dests:
             rid, pid, _ = topo.addr(d)
             ids.append(DstId(rid=rid, pnc=pid))
         sent[0] += len(engs)
-        return RemoteDMATransfer(dst_ids=ids, dma_engine_mask=_mk(engs), remote_sem=rsem, srcs=[buf[s]],
-                                 dsts=[buf[s]] * len(dests), alu_op=0)
+        return RemoteDMATransfer(dst_ids=ids, dma_engine_mask=_mk(engs), remote_sem=rsem,
+                                 srcs=[buf[slot_fn(core, s)]], dsts=[buf[slot_fn(d, s)] for d in dests], alu_op=0)
 
-    def ml_xfers(s, dests):
-        return [xfer(T.land_ml, s, part, [e], sem.ml_arr)
+    def o_sem(s):
+        return sem["o_c%d" % (gidx[s] // 2)]
+
+    if T.rank_of(core) is None:
+        for s in cores:
+            hs = helpers(s)
+            if core in hs:
+                share = unreached(s)[hs.index(core)::len(hs)]
+                g.wait_ge(sem.o_sib, NE_SO)
+                g.remote_dma_fused([xfer(T.land_o, oslot, s, share, _bits(topo.mask(core, share[0]))[0::2],
+                                         o_sem(s))], local_sem=sem.sent)
+                g.wait_ge(sem.sent, sent[0])
+        return
+
+    sib = [x for x in cores if x != core and topo.chip(x) == topo.chip(core)][0]
+    others = [d for d in cores if d != core and d != sib]
+    direct = [d for d in others if topo.may_write(core, d)]
+    passed = unreached(sib)
+    off = _bits(topo.mask(core, others[0]))
+    on_only = [e for e in _bits(topo.mask(core, sib)) if e not in off]
+    e_o = off[0::2]
+    e_m = [off[1], off[3]]
+    e_sm, e_so = [on_only[0]], on_only[0:NE_SO]
+
+    def ml_xfers(s, dests, rsem):
+        return [xfer(T.land_ml, mslot, s, part, [e], rsem)
                 for part, e in ((dests[0::2], e_m[0]), (dests[1::2], e_m[1])) if part]
 
-    g.sync.dma_start(T.land_ml[me, 0:64, :], T.ml[:]).then_inc(sem.ld_ml, 16)
-    g.scalar.dma_start(T.land_ml[me, 64:128, :], T.ml[:]).then_inc(sem.ld_ml, 16)
-    g.sync.dma_start(T.land_o[me], T.o[:]).then_inc(sem.ld_o, 16)
+    mine = order_of(core)
+    ne = n_early(core)
+    nt = N - ne
+    nec, ntc = ne // 2, nt // 2
+
+    mm_ = mslot(core, core)
+    g.sync.dma_start(T.land_ml[mm_, 0:64, :], T.ml[:]).then_inc(sem.ld_ml, 16)
+    g.scalar.dma_start(T.land_ml[mm_, 64:128, :], T.ml[:]).then_inc(sem.ld_ml, 16)
+    g.sync.dma_start(T.land_o[oslot(core, core)], T.o[:]).then_inc(sem.ld_o, 16)
 
     g.vector.memset(T.ones[:], 1.0).then_inc(sem.k_ones, 1)
     g.wait_ge(sem.k_ones, 1)
@@ -89,30 +140,26 @@ def rank_program(g, core, T, topo):
     g.vector.tensor_tensor(T.istack[:], T.ident[:, 0:64], T.ident[:, 64:128], AluOpType.add).then_inc(sem.k_is, 1)
 
     g.wait_ge(sem.ld_ml, 32)
-    g.remote_dma_fused([xfer(T.land_ml, me, [sib], e_sm, sem.ml_sib)] + ml_xfers(me, direct), local_sem=sem.sent)
+    g.remote_dma_fused([xfer(T.land_ml, mslot, core, [sib], e_sm, sem.ml_sib)] + ml_xfers(core, direct, sem.ml_arr),
+                       local_sem=sem.sent)
     g.wait_ge(sem.ld_o, 16)
-    g.remote_dma_fused([xfer(T.land_o, me, [sib], e_so, sem.o_sib),
-                        xfer(T.land_o, me, direct, e_o, sem["o_c%d" % (me // 2)])], local_sem=sem.sent)
+    g.remote_dma_fused([xfer(T.land_o, oslot, core, helpers(core) + [sib], e_so, sem.o_sib),
+                        xfer(T.land_o, oslot, core, direct, e_o, o_sem(core))], local_sem=sem.sent)
     if passed:
-        ss = slot[sib]
         g.wait_ge(sem.ml_sib, 1)
-        g.remote_dma_fused(ml_xfers(ss, passed), local_sem=sem.sent)
-        g.wait_ge(sem.o_sib, NE_SO)
-        g.remote_dma_fused([xfer(T.land_o, ss, passed, e_ro, sem["o_c%d" % (ss // 2)])], local_sem=sem.sent)
+        g.remote_dma_fused(ml_xfers(sib, passed, sem.ml_late), local_sem=sem.sent)
     g.wait_ge(sem.sent, sent[0])
 
     g.scalar.wait_ge(sem.ld_ml, 32)
     g.scalar.wait_ge(sem.ml_sib, 1)
-    g.scalar.wait_ge(sem.ml_arr, len(others))
-    g.scalar.dma_start(T.mlb[0:N, :], T.land_ml[:]).then_inc(sem.ml_in, 16)
+    g.scalar.wait_ge(sem.ml_arr, ne - 2)
+    g.scalar.dma_start(T.mlb_e[0:ne, :], T.land_ml[0:ne]).then_inc(sem.mle_in, 16)
+    g.scalar.wait_ge(sem.ml_late, nt)
+    g.scalar.dma_start(T.mlb_t[0:nt, :], T.land_ml[ne:N]).then_inc(sem.mlt_in, 16)
 
-    def late(k):
-        return any(not (s == core or topo.may_write(s, core)) for s in order[2 * k:2 * k + 2])
-
-    korder = sorted(range(NCH), key=lambda k: (late(k), k))
-    for k in korder:
+    for k in range(NCH):
         cnt = 0
-        for s in order[2 * k:2 * k + 2]:
+        for s in mine[2 * k:2 * k + 2]:
             if s == core:
                 g.sync.wait_ge(sem.ld_o, 16)
             elif s == sib:
@@ -120,54 +167,75 @@ def rank_program(g, core, T, topo):
             else:
                 cnt += NE_O if topo.may_write(s, core) else NE_RO
         if cnt:
-            g.sync.wait_ge(sem["o_c%d" % k], cnt)
+            g.sync.wait_ge(o_sem(mine[2 * k]), cnt)
         g.sync.dma_start(T.o_all[:, k * W:k * W + 128], T.land_o[2 * k:2 * k + 2]).then_inc(sem["c%d" % k], 16)
 
     g.tensor.wait_ge(sem.k_id, 1)
-    g.tensor.wait_ge(sem.ml_in, 16)
-    g.tensor.matmul(T.ps_m[:, 0:N], T.mlb[0:N, 0:256:2], T.ident[0:N, 0:N], True, True).then_inc(sem.pm, 1)
-    g.tensor.matmul(T.ps_l[:, 0:N], T.mlb[0:N, 1:256:2], T.ident[0:N, 0:N], True, True).then_inc(sem.pl, 1)
+    g.tensor.wait_ge(sem.mle_in, 16)
+    g.tensor.matmul(T.ps_me[:, 0:ne], T.mlb_e[0:ne, 0:256:2], T.ident[0:ne, 0:ne], True, True).then_inc(sem.pme, 1)
+    g.tensor.matmul(T.ps_le[:, 0:ne], T.mlb_e[0:ne, 1:256:2], T.ident[0:ne, 0:ne], True, True).then_inc(sem.ple, 1)
+    g.tensor.wait_ge(sem.mlt_in, 16)
+    g.tensor.wait_ge(sem.vme2, 1)
+    g.tensor.matmul(T.ps_mt[:, 1:1 + nt], T.mlb_t[0:nt, 0:256:2], T.ident[0:nt, 0:nt], True,
+                    True).then_inc(sem.pmt, 1)
+    g.tensor.matmul(T.ps_lt[:, 0:nt], T.mlb_t[0:nt, 1:256:2], T.ident[0:nt, 0:nt], True, True).then_inc(sem.plt, 1)
 
-    g.vector.wait_ge(sem.pm, 1)
-    g.vector.tensor_reduce(T.negm[:, 0:1], T.ps_m[:, 0:N], AxisListType.X, AluOpType.max,
-                           negate=True).then_inc(sem.vm, 1)
-    g.vector.wait_ge(sem.pl, 1)
+    g.vector.wait_ge(sem.pme, 1)
+    g.vector.tensor_reduce(T.negm_e[:, 0:1], T.ps_me[:, 0:ne], AxisListType.X, AluOpType.max,
+                           negate=True).then_inc(sem.vme, 1)
+    g.vector.wait_ge(sem.vme, 1)
+    g.vector.tensor_scalar(T.ps_mt[:, 0:1], T.negm_e[:, 0:1], -1.0, None, mult).then_inc(sem.vme2, 1)
+    g.vector.wait_ge(sem.ple, 1)
     for h in (0, 1):
-        g.vector.tensor_copy(T.o_all[64 * h:64 * h + 64, 128:NCH * W:W],
-                             T.ps_l[64 * h:64 * h + 64, h:N:2]).then_inc(sem.vl, 1)
-
-    g.scalar.wait_ge(sem.vm, 1)
+        g.vector.tensor_copy(T.o_all[64 * h:64 * h + 64, 128:nec * W:W],
+                             T.ps_le[64 * h:64 * h + 64, h * nec:(h + 1) * nec]).then_inc(sem.vle, 1)
+    g.scalar.wait_ge(sem.vme, 1)
     for h in (0, 1):
-        g.scalar.activation(T.fsel[64 * h:64 * h + 64, 0:NCH], T.ps_m[64 * h:64 * h + 64, h:N:2],
-                            ActivationFunctionType.Exp, bias=T.negm[64 * h:64 * h + 64, 0:1],
-                            scale=1.0).then_inc(sem.sf, 1)
+        g.scalar.activation(T.f_e[64 * h:64 * h + 64, 0:nec], T.ps_me[64 * h:64 * h + 64, h * nec:(h + 1) * nec],
+                            Exp, bias=T.negm_e[64 * h:64 * h + 64, 0:1], scale=1.0).then_inc(sem.sfe, 1)
 
-    g.vector.wait_ge(sem.sf, 2)
-    g.vector.wait_ge(sem.k_is, 1)
-    g.scalar.wait_ge(sem.sf, 2)
+    g.vector.wait_ge(sem.pmt, 1)
+    g.vector.tensor_reduce(T.negm[:, 0:1], T.ps_mt[:, 0:1 + nt], AxisListType.X, AluOpType.max,
+                           negate=True).then_inc(sem.vmt, 1)
+    g.vector.wait_ge(sem.plt, 1)
+    for h in (0, 1):
+        g.vector.tensor_copy(T.o_all[64 * h:64 * h + 64, nec * W + 128:NCH * W:W],
+                             T.ps_lt[64 * h:64 * h + 64, h * ntc:(h + 1) * ntc]).then_inc(sem.vlt, 1)
+    g.scalar.wait_ge(sem.vmt, 1)
+    g.scalar.activation(T.f_t[:, 0:1 + nt], T.ps_mt[:, 0:1 + nt], Exp, bias=T.negm[:, 0:1],
+                        scale=1.0).then_inc(sem.sft, 1)
+
+    g.scalar.wait_ge(sem.sft, 1)
     g.scalar.wait_ge(sem.k_is, 1)
-    for i, k in enumerate(korder):
-        a_k = T.amat[:, 64 * k:64 * k + 64]
-        if i % 2 == 0:
-            g.vector.tensor_scalar(a_k, T.istack[:], T.fsel[:, k:k + 1], None,
-                                   AluOpType.mult).then_inc(sem["a%d" % k], 1)
-        else:
-            g.scalar.activation(a_k, T.istack[:], ActivationFunctionType.Copy,
-                                scale=T.fsel[:, k:k + 1]).then_inc(sem["a%d" % k], 1)
+    for i in range(ntc):
+        k = nec + i
+        g.scalar.activation(T.amat[64:128, 64 * k:64 * k + 64], T.istack[64:128, :], Copy,
+                            scale=T.f_t[64:128, 1 + ntc + i:2 + ntc + i]).then_inc(sem["a%d" % k], 1)
+    g.vector.wait_ge(sem.sft, 1)
+    g.vector.wait_ge(sem.sfe, 2)
+    g.vector.wait_ge(sem.k_is, 1)
+    for k in range(nec):
+        g.vector.tensor_scalar(T.amat[:, 64 * k:64 * k + 64], T.istack[:], T.f_e[:, k:k + 1], T.f_t[:, 0:1], mult,
+                               mult).then_inc(sem["a%d" % k], 1)
+    for i in range(ntc):
+        k = nec + i
+        g.vector.tensor_scalar(T.amat[0:64, 64 * k:64 * k + 64], T.istack[0:64, :], T.f_t[0:64, 1 + i:2 + i], None,
+                               mult).then_inc(sem["a%d" % k], 1)
 
-    g.tensor.wait_ge(sem.vl, 2)
-    for i, k in enumerate(korder):
-        g.tensor.wait_ge(sem["a%d" % k], 1)
+    g.tensor.wait_ge(sem.vle, 2)
+    for k in range(NCH):
+        if k == nec:
+            g.tensor.wait_ge(sem.vlt, 2)
+        g.tensor.wait_ge(sem["a%d" % k], 1 if k < nec else 2)
         g.tensor.wait_ge(sem["c%d" % k], 16)
         mm = g.tensor.matmul(T.ps_y[0:Q, 0:129], T.amat[:, 64 * k:64 * k + 64], T.o_all[:, k * W:k * W + 129],
-                             i == 0, i == NCH - 1)
+                             k == 0, k == NCH - 1)
     mm.then_inc(sem.py, 1)
 
     g.vector.wait_ge(sem.py, 1)
     g.vector.reciprocal(T.rden[0:Q, 0:1], T.ps_y[0:Q, 128:129]).then_inc(sem.vr, 1)
     g.vector.wait_ge(sem.vr, 1)
-    g.vector.tensor_scalar(T.y_sb[0:Q, :], T.ps_y[0:Q, 0:128], T.rden[0:Q, 0:1], None,
-                           AluOpType.mult).then_inc(sem.vy, 1)
+    g.vector.tensor_scalar(T.y_sb[0:Q, :], T.ps_y[0:Q, 0:128], T.rden[0:Q, 0:1], None, mult).then_inc(sem.vy, 1)
     g.sync.wait_ge(sem.vy, 1)
     g.sync.dma_start(T.y[:], T.y_sb[0:Q, :]).then_inc(sem.st, 16)
     g.sync.wait_ge(sem.st, 16)

@@ -1,10 +1,12 @@
 from concourse.bass import DstId, RemoteDMATransfer
 from concourse.mybir import AluOpType, AxisListType, ActivationFunctionType
+import math
 
 N = 12
 Q = 64
 NCH = N // 2
 W = 136
+CL = 20.0
 
 SCRATCH = {
     "land_o": ("dram", [N, 128, 64], "bfloat16"),
@@ -12,7 +14,8 @@ SCRATCH = {
     "mlb_e": ("sbuf", [128, 256], "float32"),
     "mlb_t": ("sbuf", [128, 256], "float32"),
     "o_all": ("sbuf", [128, NCH * W], "bfloat16"),
-    "ones": ("sbuf", [128, 128], "float32"),
+    "pmi": ("sbuf", [128, 128], "float32"),
+    "mask": ("sbuf", [128, 128], "float32"),
     "ident": ("sbuf", [128, 128], "float32"),
     "istack": ("sbuf", [128, 64], "bfloat16"),
     "amat": ("sbuf", [128, NCH * 64], "bfloat16"),
@@ -27,10 +30,11 @@ SCRATCH = {
     "ps_mt": ("psum", [128, 512], "float32"),
     "ps_lt": ("psum", [128, 512], "float32"),
     "ps_y": ("psum", [128, 512], "float32"),
+    "ps_d": ("psum", [128, 512], "float32"),
 }
-SEMAPHORES = (["ld_ml", "ld_o", "ml_sib", "ml_arr", "ml_late", "o_sib", "sent", "k_ones", "k_id", "k_is",
+SEMAPHORES = (["ld_ml", "ld_o", "ml_sib", "ml_arr", "ml_late", "o_sib", "sent", "k_pmi", "k_mask", "k_id", "k_is",
                "mle_in", "mlt_in", "pme", "ple", "pmt", "plt", "vme", "vme2", "vle", "vmt", "vlt", "sfe",
-               "sft", "py", "vr", "vy", "st"]
+               "sft", "py", "pd", "vr", "vy", "st"]
               + ["o_c%d" % k for k in range(NCH)] + ["c%d" % k for k in range(NCH)] + ["a%d" % k for k in range(NCH)])
 
 NE_O, NE_RO, NE_SO = 4, 4, 4
@@ -133,9 +137,11 @@ def rank_program(g, core, T, topo):
     g.scalar.dma_start(T.land_ml[mm_, 64:128, :], T.ml[:]).then_inc(sem.ld_ml, 16)
     g.sync.dma_start(T.land_o[oslot(core, core)], T.o[:]).then_inc(sem.ld_o, 16)
 
-    g.vector.memset(T.ones[:], 1.0).then_inc(sem.k_ones, 1)
-    g.wait_ge(sem.k_ones, 1)
-    g.affine_select(T.ident[:], T.ones[:], [[-1, 128]], AluOpType.is_equal, 0.0, 0, 1).then_inc(sem.k_id, 1)
+    g.iota(T.pmi[:], [[-1, 128]], 0, 1, allow_small_or_imprecise_dtypes=True).then_inc(sem.k_pmi, 1)
+    g.vector.wait_ge(sem.k_pmi, 1)
+    g.vector.tensor_scalar(T.mask[:], T.pmi[:], 0.0, -1000.0, AluOpType.not_equal, mult).then_inc(sem.k_mask, 1)
+    g.scalar.wait_ge(sem.k_mask, 1)
+    g.scalar.activation(T.ident[:], T.mask[:], Exp).then_inc(sem.k_id, 1)
     g.vector.wait_ge(sem.k_id, 1)
     g.vector.tensor_tensor(T.istack[:], T.ident[:, 0:64], T.ident[:, 64:128], AluOpType.add).then_inc(sem.k_is, 1)
 
@@ -184,7 +190,7 @@ def rank_program(g, core, T, topo):
     g.vector.tensor_reduce(T.negm_e[:, 0:1], T.ps_me[:, 0:ne], AxisListType.X, AluOpType.max,
                            negate=True).then_inc(sem.vme, 1)
     g.vector.wait_ge(sem.vme, 1)
-    g.vector.tensor_scalar(T.ps_mt[:, 0:1], T.negm_e[:, 0:1], -1.0, None, mult).then_inc(sem.vme2, 1)
+    g.vector.tensor_scalar(T.ps_mt[:, 0:1], T.negm_e[:, 0:1], -1.0, CL, mult, AluOpType.add).then_inc(sem.vme2, 1)
     g.vector.wait_ge(sem.ple, 1)
     for h in (0, 1):
         g.vector.tensor_copy(T.o_all[64 * h:64 * h + 64, 128:nec * W:W],
@@ -193,6 +199,11 @@ def rank_program(g, core, T, topo):
     for h in (0, 1):
         g.scalar.activation(T.f_e[64 * h:64 * h + 64, 0:nec], T.ps_me[64 * h:64 * h + 64, h * nec:(h + 1) * nec],
                             Exp, bias=T.negm_e[64 * h:64 * h + 64, 0:1], scale=1.0).then_inc(sem.sfe, 1)
+    g.vector.wait_ge(sem.sfe, 2)
+    g.vector.wait_ge(sem.k_is, 1)
+    for k in range(nec):
+        g.vector.tensor_scalar(T.amat[:, 64 * k:64 * k + 64], T.istack[:], T.f_e[:, k:k + 1], math.exp(-CL), mult,
+                               mult).then_inc(sem["a%d" % k], 1)
 
     g.vector.wait_ge(sem.pmt, 1)
     g.vector.tensor_reduce(T.negm[:, 0:1], T.ps_mt[:, 0:1 + nt], AxisListType.X, AluOpType.max,
@@ -202,7 +213,7 @@ def rank_program(g, core, T, topo):
         g.vector.tensor_copy(T.o_all[64 * h:64 * h + 64, nec * W + 128:NCH * W:W],
                              T.ps_lt[64 * h:64 * h + 64, h * ntc:(h + 1) * ntc]).then_inc(sem.vlt, 1)
     g.scalar.wait_ge(sem.vmt, 1)
-    g.scalar.activation(T.f_t[:, 0:1 + nt], T.ps_mt[:, 0:1 + nt], Exp, bias=T.negm[:, 0:1],
+    g.scalar.activation(T.f_t[:, 1:1 + nt], T.ps_mt[:, 1:1 + nt], Exp, bias=T.negm[:, 0:1],
                         scale=1.0).then_inc(sem.sft, 1)
 
     g.scalar.wait_ge(sem.sft, 1)
@@ -212,29 +223,39 @@ def rank_program(g, core, T, topo):
         g.scalar.activation(T.amat[64:128, 64 * k:64 * k + 64], T.istack[64:128, :], Copy,
                             scale=T.f_t[64:128, 1 + ntc + i:2 + ntc + i]).then_inc(sem["a%d" % k], 1)
     g.vector.wait_ge(sem.sft, 1)
-    g.vector.wait_ge(sem.sfe, 2)
-    g.vector.wait_ge(sem.k_is, 1)
-    for k in range(nec):
-        g.vector.tensor_scalar(T.amat[:, 64 * k:64 * k + 64], T.istack[:], T.f_e[:, k:k + 1], T.f_t[:, 0:1], mult,
-                               mult).then_inc(sem["a%d" % k], 1)
     for i in range(ntc):
         k = nec + i
         g.vector.tensor_scalar(T.amat[0:64, 64 * k:64 * k + 64], T.istack[0:64, :], T.f_t[0:64, 1 + i:2 + i], None,
                                mult).then_inc(sem["a%d" % k], 1)
 
-    g.tensor.wait_ge(sem.vle, 2)
-    for k in range(NCH):
-        if k == nec:
-            g.tensor.wait_ge(sem.vlt, 2)
+    def den_mm(k):
         g.tensor.wait_ge(sem["a%d" % k], 1 if k < nec else 2)
+        return g.tensor.matmul(T.ps_d[0:Q, 0:1], T.amat[:, 64 * k:64 * k + 64],
+                               T.o_all[:, k * W + 128:k * W + 129], k == 0, k == NCH - 1)
+
+    def num_mm(k):
         g.tensor.wait_ge(sem["c%d" % k], 16)
-        mm = g.tensor.matmul(T.ps_y[0:Q, 0:129], T.amat[:, 64 * k:64 * k + 64], T.o_all[:, k * W:k * W + 129],
-                             k == 0, k == NCH - 1)
+        return g.tensor.matmul(T.ps_y[0:Q, 0:128], T.amat[:, 64 * k:64 * k + 64], T.o_all[:, k * W:k * W + 128],
+                               k == 0, k == NCH - 1)
+
+    split = max(nec - 2, 0)
+    g.tensor.wait_ge(sem.vle, 2)
+    for k in range(nec):
+        den_mm(k)
+    for k in range(split):
+        num_mm(k)
+    g.tensor.wait_ge(sem.vlt, 2)
+    for k in range(nec, NCH):
+        mm = den_mm(k)
+    mm.then_inc(sem.pd, 1)
+    for k in range(split, NCH):
+        mm = num_mm(k)
     mm.then_inc(sem.py, 1)
 
-    g.vector.wait_ge(sem.py, 1)
-    g.vector.reciprocal(T.rden[0:Q, 0:1], T.ps_y[0:Q, 128:129]).then_inc(sem.vr, 1)
+    g.vector.wait_ge(sem.pd, 1)
+    g.vector.reciprocal(T.rden[0:Q, 0:1], T.ps_d[0:Q, 0:1]).then_inc(sem.vr, 1)
     g.vector.wait_ge(sem.vr, 1)
+    g.vector.wait_ge(sem.py, 1)
     g.vector.tensor_scalar(T.y_sb[0:Q, :], T.ps_y[0:Q, 0:128], T.rden[0:Q, 0:1], None, mult).then_inc(sem.vy, 1)
     g.sync.wait_ge(sem.vy, 1)
     g.sync.dma_start(T.y[:], T.y_sb[0:Q, :]).then_inc(sem.st, 16)

from concourse.bass import DstId, RemoteDMATransfer
from concourse.mybir import AluOpType, AxisListType, ActivationFunctionType
import math

N = 12
Q = 64
NCH = N // 2
W = 136
CL = 20.0

SCRATCH = {
    "land_o": ("dram", [N, 128, 64], "bfloat16"),
    "land_ml": ("dram", [N, 128, 2], "float32"),
    "mlb_e": ("sbuf", [128, 256], "float32"),
    "mlb_t": ("sbuf", [128, 256], "float32"),
    "o_all": ("sbuf", [128, NCH * W], "bfloat16"),
    "pmi": ("sbuf", [128, 128], "float32"),
    "mask": ("sbuf", [128, 128], "float32"),
    "ident": ("sbuf", [128, 128], "float32"),
    "istack": ("sbuf", [128, 64], "bfloat16"),
    "amat": ("sbuf", [128, NCH * 64], "bfloat16"),
    "negm_e": ("sbuf", [128, 1], "float32"),
    "negm": ("sbuf", [128, 1], "float32"),
    "f_e": ("sbuf", [128, 8], "float32"),
    "f_t": ("sbuf", [128, 8], "float32"),
    "rden": ("sbuf", [128, 1], "float32"),
    "y_sb": ("sbuf", [128, 128], "bfloat16"),
    "ps_me": ("psum", [128, 512], "float32"),
    "ps_le": ("psum", [128, 512], "float32"),
    "ps_mt": ("psum", [128, 512], "float32"),
    "ps_lt": ("psum", [128, 512], "float32"),
    "ps_y": ("psum", [128, 512], "float32"),
    "ps_d": ("psum", [128, 512], "float32"),
}
SEMAPHORES = (["ld_ml", "ld_o", "ml_sib", "ml_arr", "ml_late", "o_sib", "sent", "k_pmi", "k_mask", "k_id", "k_is",
               "mle_in", "mlt_in", "pme", "ple", "pmt", "plt", "vme", "vme2", "vle", "vmt", "vlt", "sfe",
               "sft", "py", "pd", "vr", "vy", "st"]
              + ["o_c%d" % k for k in range(NCH)] + ["c%d" % k for k in range(NCH)] + ["a%d" % k for k in range(NCH)])

NE_O, NE_RO, NE_SO = 4, 4, 4
NHELP = 2


def _bits(mask):
    return [e for e in range(mask.bit_length()) if (mask >> e) & 1]


def _mk(engs):
    return sum(1 << e for e in engs)


def rank_program(g, core, T, topo):
    cores = list(T.cores)
    sem = T.sem
    Exp, Copy = ActivationFunctionType.Exp, ActivationFunctionType.Copy
    mult = AluOpType.mult

    def hop1(s, d):
        return bool(s == d or topo.may_write(s, d))

    gorder = sorted(cores, key=lambda s: (tuple(hop1(s, d) for d in cores), cores.index(s)))
    gidx = {s: i for i, s in enumerate(gorder)}

    def order_of(d):
        return sorted(cores, key=lambda s: (not hop1(s, d), gidx[s]))

    def n_early(d):
        return sum(1 for s in cores if hop1(s, d))

    def oslot(d, s):
        return order_of(d).index(s) if d in cores else 0

    def mslot(d, s):
        j, ne = oslot(d, s), n_early(d)
        if j < ne:
            return (j % 2) * (ne // 2) + j // 2
        j -= ne
        return ne + (j % 2) * ((N - ne) // 2) + j // 2

    def unreached(s):
        return [d for d in cores if not hop1(s, d)]

    def helpers(s):
        far = unreached(s)
        if not far:
            return []
        return [c for c in range(topo.CORES_PER_CHIP * topo.CHIPS)
                if c not in cores and topo.chip(c) == topo.chip(s) and topo.die(c) == topo.die(s)
                and all(topo.may_write(c, d) for d in far)][:NHELP]

    sent = [0]

    def xfer(buf, slot_fn, s, dests, engs, rsem):
        ids = []
        for d in dests:
            rid, pid, _ = topo.addr(d)
            ids.append(DstId(rid=rid, pnc=pid))
        sent[0] += len(engs)
        return RemoteDMATransfer(dst_ids=ids, dma_engine_mask=_mk(engs), remote_sem=rsem,
                                 srcs=[buf[slot_fn(core, s)]], dsts=[buf[slot_fn(d, s)] for d in dests], alu_op=0)

    def o_sem(s):
        return sem["o_c%d" % (gidx[s] // 2)]

    if T.rank_of(core) is None:
        for s in cores:
            hs = helpers(s)
            if core in hs:
                share = unreached(s)[hs.index(core)::len(hs)]
                g.wait_ge(sem.o_sib, NE_SO)
                g.remote_dma_fused([xfer(T.land_o, oslot, s, share, _bits(topo.mask(core, share[0]))[0::2],
                                         o_sem(s))], local_sem=sem.sent)
                g.wait_ge(sem.sent, sent[0])
        return

    sib = [x for x in cores if x != core and topo.chip(x) == topo.chip(core)][0]
    others = [d for d in cores if d != core and d != sib]
    direct = [d for d in others if topo.may_write(core, d)]
    passed = unreached(sib)
    off = _bits(topo.mask(core, others[0]))
    on_only = [e for e in _bits(topo.mask(core, sib)) if e not in off]
    e_o = off[0::2]
    e_m = [off[1], off[3]]
    e_sm, e_so = [on_only[0]], on_only[0:NE_SO]

    def ml_xfers(s, dests, rsem):
        return [xfer(T.land_ml, mslot, s, part, [e], rsem)
                for part, e in ((dests[0::2], e_m[0]), (dests[1::2], e_m[1])) if part]

    mine = order_of(core)
    ne = n_early(core)
    nt = N - ne
    nec, ntc = ne // 2, nt // 2

    mm_ = mslot(core, core)
    g.sync.dma_start(T.land_ml[mm_, 0:64, :], T.ml[:]).then_inc(sem.ld_ml, 16)
    g.scalar.dma_start(T.land_ml[mm_, 64:128, :], T.ml[:]).then_inc(sem.ld_ml, 16)
    g.sync.dma_start(T.land_o[oslot(core, core)], T.o[:]).then_inc(sem.ld_o, 16)

    g.iota(T.pmi[:], [[-1, 128]], 0, 1, allow_small_or_imprecise_dtypes=True).then_inc(sem.k_pmi, 1)
    g.vector.wait_ge(sem.k_pmi, 1)
    g.vector.tensor_scalar(T.mask[:], T.pmi[:], 0.0, -1000.0, AluOpType.not_equal, mult).then_inc(sem.k_mask, 1)
    g.scalar.wait_ge(sem.k_mask, 1)
    g.scalar.activation(T.ident[:], T.mask[:], Exp).then_inc(sem.k_id, 1)
    g.vector.wait_ge(sem.k_id, 1)
    g.vector.tensor_tensor(T.istack[:], T.ident[:, 0:64], T.ident[:, 64:128], AluOpType.add).then_inc(sem.k_is, 1)

    g.wait_ge(sem.ld_ml, 32)
    g.remote_dma_fused([xfer(T.land_ml, mslot, core, [sib], e_sm, sem.ml_sib)] + ml_xfers(core, direct, sem.ml_arr),
                       local_sem=sem.sent)
    g.wait_ge(sem.ld_o, 16)
    g.remote_dma_fused([xfer(T.land_o, oslot, core, helpers(core) + [sib], e_so, sem.o_sib),
                        xfer(T.land_o, oslot, core, direct, e_o, o_sem(core))], local_sem=sem.sent)
    if passed:
        g.wait_ge(sem.ml_sib, 1)
        g.remote_dma_fused(ml_xfers(sib, passed, sem.ml_late), local_sem=sem.sent)
    g.wait_ge(sem.sent, sent[0])

    g.scalar.wait_ge(sem.ld_ml, 32)
    g.scalar.wait_ge(sem.ml_sib, 1)
    g.scalar.wait_ge(sem.ml_arr, ne - 2)
    g.scalar.dma_start(T.mlb_e[0:ne, :], T.land_ml[0:ne]).then_inc(sem.mle_in, 16)
    g.scalar.wait_ge(sem.ml_late, nt)
    g.scalar.dma_start(T.mlb_t[0:nt, :], T.land_ml[ne:N]).then_inc(sem.mlt_in, 16)

    for k in range(NCH):
        cnt = 0
        for s in mine[2 * k:2 * k + 2]:
            if s == core:
                g.sync.wait_ge(sem.ld_o, 16)
            elif s == sib:
                g.sync.wait_ge(sem.o_sib, NE_SO)
            else:
                cnt += NE_O if topo.may_write(s, core) else NE_RO
        if cnt:
            g.sync.wait_ge(o_sem(mine[2 * k]), cnt)
        g.sync.dma_start(T.o_all[:, k * W:k * W + 128], T.land_o[2 * k:2 * k + 2]).then_inc(sem["c%d" % k], 16)

    g.tensor.wait_ge(sem.k_id, 1)
    g.tensor.wait_ge(sem.mle_in, 16)
    g.tensor.matmul(T.ps_me[:, 0:ne], T.mlb_e[0:ne, 0:256:2], T.ident[0:ne, 0:ne], True, True).then_inc(sem.pme, 1)
    g.tensor.matmul(T.ps_le[:, 0:ne], T.mlb_e[0:ne, 1:256:2], T.ident[0:ne, 0:ne], True, True).then_inc(sem.ple, 1)
    g.tensor.wait_ge(sem.mlt_in, 16)
    g.tensor.wait_ge(sem.vme2, 1)
    g.tensor.matmul(T.ps_mt[:, 1:1 + nt], T.mlb_t[0:nt, 0:256:2], T.ident[0:nt, 0:nt], True,
                    True).then_inc(sem.pmt, 1)
    g.tensor.matmul(T.ps_lt[:, 0:nt], T.mlb_t[0:nt, 1:256:2], T.ident[0:nt, 0:nt], True, True).then_inc(sem.plt, 1)

    g.vector.wait_ge(sem.pme, 1)
    g.vector.tensor_reduce(T.negm_e[:, 0:1], T.ps_me[:, 0:ne], AxisListType.X, AluOpType.max,
                           negate=True).then_inc(sem.vme, 1)
    g.vector.wait_ge(sem.vme, 1)
    g.vector.tensor_scalar(T.ps_mt[:, 0:1], T.negm_e[:, 0:1], -1.0, CL, mult, AluOpType.add).then_inc(sem.vme2, 1)
    g.vector.wait_ge(sem.ple, 1)
    for h in (0, 1):
        g.vector.tensor_copy(T.o_all[64 * h:64 * h + 64, 128:nec * W:W],
                             T.ps_le[64 * h:64 * h + 64, h * nec:(h + 1) * nec]).then_inc(sem.vle, 1)
    g.scalar.wait_ge(sem.vme, 1)
    for h in (0, 1):
        g.scalar.activation(T.f_e[64 * h:64 * h + 64, 0:nec], T.ps_me[64 * h:64 * h + 64, h * nec:(h + 1) * nec],
                            Exp, bias=T.negm_e[64 * h:64 * h + 64, 0:1], scale=1.0).then_inc(sem.sfe, 1)
    g.vector.wait_ge(sem.sfe, 2)
    g.vector.wait_ge(sem.k_is, 1)
    for k in range(nec):
        g.vector.tensor_scalar(T.amat[:, 64 * k:64 * k + 64], T.istack[:], T.f_e[:, k:k + 1], math.exp(-CL), mult,
                               mult).then_inc(sem["a%d" % k], 1)

    g.vector.wait_ge(sem.pmt, 1)
    g.vector.tensor_reduce(T.negm[:, 0:1], T.ps_mt[:, 0:1 + nt], AxisListType.X, AluOpType.max,
                           negate=True).then_inc(sem.vmt, 1)
    g.vector.wait_ge(sem.plt, 1)
    for h in (0, 1):
        g.vector.tensor_copy(T.o_all[64 * h:64 * h + 64, nec * W + 128:NCH * W:W],
                             T.ps_lt[64 * h:64 * h + 64, h * ntc:(h + 1) * ntc]).then_inc(sem.vlt, 1)
    g.scalar.wait_ge(sem.vmt, 1)
    g.scalar.activation(T.f_t[:, 1:1 + nt], T.ps_mt[:, 1:1 + nt], Exp, bias=T.negm[:, 0:1],
                        scale=1.0).then_inc(sem.sft, 1)

    g.scalar.wait_ge(sem.sft, 1)
    g.scalar.wait_ge(sem.k_is, 1)
    for i in range(ntc):
        k = nec + i
        g.scalar.activation(T.amat[64:128, 64 * k:64 * k + 64], T.istack[64:128, :], Copy,
                            scale=T.f_t[64:128, 1 + ntc + i:2 + ntc + i]).then_inc(sem["a%d" % k], 1)
    g.vector.wait_ge(sem.sft, 1)
    for i in range(ntc):
        k = nec + i
        g.vector.tensor_scalar(T.amat[0:64, 64 * k:64 * k + 64], T.istack[0:64, :], T.f_t[0:64, 1 + i:2 + i], None,
                               mult).then_inc(sem["a%d" % k], 1)

    def den_mm(k):
        g.tensor.wait_ge(sem["a%d" % k], 1 if k < nec else 2)
        return g.tensor.matmul(T.ps_d[0:Q, 0:1], T.amat[:, 64 * k:64 * k + 64],
                               T.o_all[:, k * W + 128:k * W + 129], k == 0, k == NCH - 1)

    def num_mm(k):
        g.tensor.wait_ge(sem["c%d" % k], 16)
        return g.tensor.matmul(T.ps_y[0:Q, 0:128], T.amat[:, 64 * k:64 * k + 64], T.o_all[:, k * W:k * W + 128],
                               k == 0, k == NCH - 1)

    split = max(nec - 2, 0)
    g.tensor.wait_ge(sem.vle, 2)
    for k in range(nec):
        den_mm(k)
    for k in range(split):
        num_mm(k)
    g.tensor.wait_ge(sem.vlt, 2)
    for k in range(nec, NCH):
        mm = den_mm(k)
    mm.then_inc(sem.pd, 1)
    for k in range(split, NCH):
        mm = num_mm(k)
    mm.then_inc(sem.py, 1)

    g.vector.wait_ge(sem.pd, 1)
    g.vector.reciprocal(T.rden[0:Q, 0:1], T.ps_d[0:Q, 0:1]).then_inc(sem.vr, 1)
    g.vector.wait_ge(sem.vr, 1)
    g.vector.wait_ge(sem.py, 1)
    g.vector.tensor_scalar(T.y_sb[0:Q, :], T.ps_y[0:Q, 0:128], T.rden[0:Q, 0:1], None, mult).then_inc(sem.vy, 1)
    g.sync.wait_ge(sem.vy, 1)
    g.sync.dma_start(T.y[:], T.y_sb[0:Q, :]).then_inc(sem.st, 16)
    g.sync.wait_ge(sem.st, 16)
